import numpy as np
import ml_dtypes


def mxq(x, axis, fmt="e4m3"):
    dtype, down = {"e4m3": (ml_dtypes.float8_e4m3fn, 7), "e5m2": (ml_dtypes.float8_e5m2, 14)}[fmt]
    v = np.moveaxis(np.asarray(x, np.float32).astype(ml_dtypes.bfloat16).astype(np.float64), axis, -1)
    blocks = v.reshape(v.shape[:-1] + (-1, 32))
    amax = np.abs(blocks).max(-1, keepdims=True)
    byte = np.maximum(np.where(amax > 0, np.frexp(amax)[1] - 1 + 127, 0) - down, 1)
    scale = np.exp2(byte - 127.0)
    codes = (blocks / scale).astype(np.float32).astype(dtype).astype(np.float64)
    return np.moveaxis((codes * scale).reshape(v.shape), -1, axis)


WIDE = False


def mx_kscale(k):
    if not WIDE:
        return np.ones(k)
    levels = np.array([30, -30])
    if k % 512:
        return np.exp2(np.random.permutation(np.resize(levels, k // 32))).repeat(32)
    a = np.empty((k // 512, 16))
    for p in range(k // 512):
        a[p, :8] = np.random.permutation(np.resize(levels, 8))
        for g in range(8):
            far = levels[np.abs(levels - a[p, g]) >= 10]
            a[p, g + 8] = far[np.random.randint(len(far))]
    return np.exp2(a.ravel()).repeat(32)


def f64(x):
    return np.asarray(x).astype(np.float64)


def striped(idx):
    return np.tile(np.asarray(idx).reshape(-1, 16).T, (8, 1)).astype(np.uint16)


def unstriped(offs):
    return offs[:16].T.reshape(-1).astype(np.int64)


E2M1 = np.array([0.0, 0.5, 1.0, 1.5, 2.0, 3.0, 4.0, 6.0, -0.0, -0.5, -1.0, -1.5, -2.0, -3.0, -4.0, -6.0])


def pack_weight(w, fmt):
    k, n = w.shape
    w = f64(np.asarray(w, np.float32).astype(ml_dtypes.bfloat16)).reshape(k // 32, 32, n)
    amax = np.abs(w).max(1)
    if fmt in ("e4m3", "e5m2"):
        byte = np.frexp(amax)[1] - 1 + 127 - (7 if fmt == "e4m3" else 14)
    else:
        mant, ex = np.frexp(amax / 6.0)
        byte = np.where(mant > 0.5, ex, ex - 1) + 127
    byte = np.clip(np.where(amax > 0, byte, 1), 1, 254)
    scaled = (w * np.exp2(127.0 - byte)[:, None, :]).reshape(k, n).astype(np.float32)
    by_word = np.ascontiguousarray(scaled.reshape(k // 512, 128, 4, n).transpose(0, 1, 3, 2))
    if fmt in ("e4m3", "e5m2"):
        words = by_word.astype(ml_dtypes.float8_e4m3fn if fmt == "e4m3" else ml_dtypes.float8_e5m2).view(np.uint8)
    else:
        c = by_word.astype(ml_dtypes.float4_e2m1fn).view(np.uint8) & 0xF
        words = (c[..., 0::2] | (c[..., 1::2] << 4)).reshape(k // 512, 128, 2 * n)
    return np.ascontiguousarray(words), np.ascontiguousarray(byte.astype(np.uint8).reshape(k // 512, 16, n))


def unpack_weight(words, scales, fmt):
    g, _, n = scales.shape
    words = np.ascontiguousarray(words).reshape(g, 128, n, -1)
    if fmt in ("e4m3", "e5m2"):
        vals = words.view(ml_dtypes.float8_e4m3fn if fmt == "e4m3" else ml_dtypes.float8_e5m2).astype(np.float64)
    else:
        nib = np.empty((g, 128, n, 4), np.uint8)
        nib[..., 0::2] = words & 0xF
        nib[..., 1::2] = words >> 4
        vals = E2M1[nib]
    vals = vals * np.repeat(np.exp2(scales.astype(np.float64) - 127.0), 8, axis=1)[..., None]
    return vals.transpose(0, 1, 3, 2).reshape(g * 512, n)


K, T, J, R, N = 512, 1024, 256, 512, 256


def setup_inputs():
    n = np.random.standard_normal
    idx = np.random.permutation(T)[:J]
    fk = mx_kscale(K)
    fr = mx_kscale(R)
    wp = pack_weight(n((K, R)) * 1 / np.sqrt(K) * fk[:, None] * fr, "e2m1")
    wbp = pack_weight(n((R, N)) * 1 / np.sqrt(R) / fr[:, None], "e5m2")
    return {
        "xf": (n((K, T))).astype(np.float32),
        "fk": (np.random.uniform(0.5, 2.0, (K, 1)) / fk[:, None]).astype(np.float32),
        "w_words": wp[0],
        "w_scales": wp[1],
        "wb_words": wbp[0],
        "wb_scales": wbp[1],
        "bi": (np.random.uniform(-0.5, 0.5, (1, N))).astype(np.float32),
        "offs": striped(idx),
    }


def reference(xf, fk, w_words, w_scales, wb_words, wb_scales, bi, offs):
    idx = unstriped(offs)
    wu = unpack_weight(w_words, w_scales, "e2m1")
    wbu = unpack_weight(wb_words, wb_scales, "e5m2")
    xg = f64(xf)[:, idx]
    x1 = np.pad(xg, ((0, 0), (1, 0)))[:, :J]
    u = (xg - 0.6 * x1) * f64(fk)
    uq = mxq(u, 0, "e4m3")
    a = wu.T @ uq
    hid = np.maximum(a, 0.0)
    hidq = mxq(hid, 0, "e5m2")
    p = hidq.T @ wbu
    ea = np.exp(0.7 * p + f64(bi))
    y = 256.0 * ea / np.sum(ea, axis=1, keepdims=True)
    return y

@@ -1,0 +1,151 @@
+from contextlib import ExitStack
+
+import concourse.mybir as mybir
+from concourse.masks import make_identity
+
+K, T, J, R, N = 512, 1024, 256, 512, 256
+FLOPS = 2 * K * R * J + 2 * R * J * N
+
+F32 = mybir.dt.float32
+BF16 = mybir.dt.bfloat16
+I32 = mybir.dt.int32
+U32 = mybir.dt.uint32
+U16 = mybir.dt.uint16
+U8 = mybir.dt.uint8
+E4M3X4 = mybir.dt.float8_e4m3fn_x4
+E5M2X4 = mybir.dt.float8_e5m2_x4
+E2M1X4 = mybir.dt.float4_e2m1fn_x4
+ALU = mybir.AluOpType
+ACT = mybir.ActivationFunctionType
+AXIS = mybir.AxisListType
+
+P = 128
+PACK = 4
+HALF = 128
+HALVES = J // HALF
+LEAD = 8
+QUADS = 4
+
+
+def tile_list_steps_plain_rowshares_kernel(tc, xf, fk, w_words, w_scales, wb_words, wb_scales, bi, offs, out):
+    nc = tc.nc
+    with ExitStack() as ctx:
+        sb = ctx.enter_context(tc.tile_pool(name="sb", bufs=1))
+        ps = ctx.enter_context(tc.psum_pool(name="ps", bufs=1))
+
+        offsets = sb.tile([P, J // 16], U16, name="offsets")
+        planes = [sb.tile([P, T], F32, name="plane%d" % t, align_bytes=64) for t in range(PACK)]
+        fk_sb = sb.tile([P, PACK], F32, name="fk_sb")
+        bi_col = sb.tile([P, 2], F32, name="bi_col")
+        w_raw = sb.tile([P, R], U16, name="w_raw", tag="words_in", align_bytes=64)
+        sc_rows = sb.tile([P, R], U8, name="sc_rows", align_bytes=64)
+        zero = sb.tile([P, PACK], F32, name="zero")
+        w_codes = sb.tile([P, R], U16, name="w_codes", align_bytes=64)
+        w_sc = sb.tile([P, R], U8, name="w_sc", align_bytes=64)
+        ident = sb.tile([P, P], F32, name="ident", align_bytes=64)
+        bias = sb.tile([P, N], F32, name="bias", align_bytes=64)
+        picked_all = sb.tile([P, PACK, LEAD + J], F32, name="picked", align_bytes=64)
+        picked = [picked_all[:, t, :] for t in range(PACK)]
+        steps = [sb.tile([P, J], F32, name="steps%d" % t, align_bytes=64) for t in range(PACK)]
+        u_bf = [sb.tile([P, HALF * PACK], BF16, name="u_bf%d" % h, align_bytes=64) for h in range(HALVES)]
+        u_codes = [sb.tile([P, HALF], U32, name="u_codes%d" % h, align_bytes=64) for h in range(HALVES)]
+        u_sc = [sb.tile([P, HALF], U8, name="u_sc%d" % h, align_bytes=64) for h in range(HALVES)]
+        hid_bf = [sb.tile([P, HALF * PACK], BF16, name="hid_bf%d" % h, align_bytes=64) for h in range(HALVES)]
+        hid_codes = [sb.tile([P, HALF], U32, name="hid_codes%d" % h, align_bytes=64) for h in range(HALVES)]
+        hid_sc = [sb.tile([P, HALF], U8, name="hid_sc%d" % h, align_bytes=64) for h in range(HALVES)]
+        neg_z = [sb.tile([P, N], F32, name="neg_z%d" % h, align_bytes=64) for h in range(HALVES)]
+        ea = [sb.tile([P, N], F32, name="ea%d" % h, align_bytes=64) for h in range(HALVES)]
+        y = [sb.tile([P, N], F32, name="y%d" % h, align_bytes=64) for h in range(HALVES)]
+        neg_max = [sb.tile([P, 1], F32, name="neg_max%d" % h) for h in range(HALVES)]
+        total = [sb.tile([P, 1], F32, name="total%d" % h) for h in range(HALVES)]
+        inv = [sb.tile([P, 1], F32, name="inv%d" % h) for h in range(HALVES)]
+        bias_ps = ps.tile([P, 2, P], F32, name="bias_ps")
+        a_ps = [ps.tile([P, PACK, HALF], F32, name="a_ps%d" % h) for h in range(HALVES)]
+        p_ps = [ps.tile([P, N], F32, name="p_ps%d" % h) for h in range(HALVES)]
+
+        xf_planes = xf.rearrange("(p t) n -> t p n", t=PACK)
+
+        nc.vector.memset(sc_rows[:].bitcast(I32), 0)
+        nc.vector.memset(zero[:], 0.0)
+
+        nc.sync.dma_start(offsets[:], offs)
+        nc.scalar.dma_start(fk_sb[:], fk.rearrange("(p t) o -> p (t o)", t=PACK))
+        nc.sync.dma_start(w_raw[:].bitcast(I32), w_words[0].bitcast(I32))
+        nc.sync.dma_start(planes[0][:], xf_planes[0])
+        nc.sync.dma_start(planes[1][:], xf_planes[1])
+        for q in range(QUADS):
+            nc.sync.dma_start(sc_rows[32 * q : 32 * q + 4, :].bitcast(I32), w_scales[0, 4 * q : 4 * q + 4, :].bitcast(I32))
+        for t in range(2, PACK):
+            nc.sync.dma_start(planes[t][:], xf_planes[t])
+        nc.sync.dma_start(bi_col[:], bi.rearrange("o (p c) -> (o p) c", c=2))
+
+        nc.scalar.activation(picked_all[:, :, LEAD - 1], zero[:], ACT.Copy)
+        make_identity(nc, ident[:])
+
+        nc.vector.tensor_copy(w_codes[:].rearrange("p (t m) -> p t m", t=PACK), w_raw[:].rearrange("p (m t) -> p t m", t=PACK))
+        nc.vector.tensor_copy(w_sc[:].rearrange("p (t m) -> p t m", t=PACK), sc_rows[:].rearrange("p (m t) -> p t m", t=PACK))
+
+        wb_codes = sb.tile([P, N], U32, name="wb_codes", tag="words_in", align_bytes=64)
+        wb_sc = sc_rows[:, 0:N]
+        nc.sync.dma_start(wb_codes[:].bitcast(I32), wb_words[0].rearrange("p n t -> p (n t)").bitcast(I32))
+        for q in range(QUADS):
+            nc.sync.dma_start(sc_rows[32 * q : 32 * q + 4, 0:N].bitcast(I32), wb_scales[0, 4 * q : 4 * q + 4, :].bitcast(I32))
+
+        for c in range(2):
+            nc.tensor.transpose(bias_ps[:, c, :], bi_col[:, c : c + 1].to_broadcast([P, P]), ident[:])
+
+        def gather(t, engine, lo, hi):
+            dst = picked[t][:, LEAD + lo : LEAD + hi]
+            src = planes[t][:].indirect(offsets[:, lo // 16 : hi // 16])
+            if engine == "scalar":
+                nc.scalar.activation(dst, src, ACT.Copy)
+            else:
+                nc.vector.tensor_copy(dst, src)
+
+        def take_steps(t, lo, hi):
+            nc.vector.scalar_tensor_tensor(
+                steps[t][:, lo:hi], picked[t][:, LEAD - 1 + lo : LEAD - 1 + hi], -0.6,
+                picked[t][:, LEAD + lo : LEAD + hi], ALU.mult, ALU.add)
+
+        def scale_round(t, h):
+            nc.vector.tensor_scalar(
+                u_bf[h][:].rearrange("p (j t) -> p j t", t=PACK)[:, :, t], steps[t][:, h * HALF : (h + 1) * HALF],
+                fk_sb[:, t : t + 1], None, ALU.mult)
+
+        for t in range(PACK - 1):
+            gather(t, "scalar", 0, J)
+            take_steps(t, 0, J)
+            for h in range(HALVES):
+                scale_round(t, h)
+        last = PACK - 1
+        gather(last, "vector", 0, HALF)
+        gather(last, "scalar", HALF, J)
+        nc.scalar.copy(bias[:].rearrange("p (n c) -> p n c", c=2), bias_ps[:].rearrange("p c n -> p n c"))
+        for h in range(HALVES):
+            take_steps(last, h * HALF, (h + 1) * HALF)
+        for h in range(HALVES):
+            scale_round(last, h)
+        for h in range(HALVES):
+            nc.vector.quantize_mx(out=u_codes[h][:].bitcast(E4M3X4), scales=u_sc[h][:], in_=u_bf[h][:])
+        for h in range(HALVES):
+            for t in range(PACK):
+                cols = slice(t * P, (t + 1) * P)
+                nc.tensor.matmul_mx(
+                    a_ps[h][:, t, :], lhsT=w_codes[:, cols].bitcast(E2M1X4), lhsT_scale=w_sc[:, cols],
+                    rhs=u_codes[h][:].bitcast(E4M3X4), rhs_scale=u_sc[h][:], start=True, stop=True)
+        for h in range(HALVES):
+            nc.scalar.activation(
+                hid_bf[h][:].rearrange("p (j t) -> p j t", t=PACK), a_ps[h][:].rearrange("p t j -> p j t"), ACT.Relu)
+        for h in range(HALVES):
+            nc.vector.quantize_mx(out=hid_codes[h][:].bitcast(E5M2X4), scales=hid_sc[h][:], in_=hid_bf[h][:])
+            nc.tensor.matmul_mx(
+                p_ps[h][:], lhsT=hid_codes[h][:].bitcast(E5M2X4), lhsT_scale=hid_sc[h][:],
+                rhs=wb_codes[:].bitcast(E5M2X4), rhs_scale=wb_sc, start=True, stop=True)
+        for h in range(HALVES):
+            nc.vector.scalar_tensor_tensor(neg_z[h][:], p_ps[h][:], -0.7, bias[:], ALU.mult, ALU.subtract)
+            nc.vector.tensor_reduce(neg_max[h][:], neg_z[h][:], AXIS.X, ALU.min)
+            nc.scalar.activation(ea[h][:], neg_z[h][:], ACT.Exp, bias=neg_max[h][:], scale=-1.0, accum_out=total[h][:])
+        for h in range(HALVES):
+            nc.vector.reciprocal(inv[h][:], total[h][:])
+            nc.vector.tensor_scalar(y[h][:], ea[h][:], inv[h][:], 256.0, ALU.mult, ALU.mult)
+            nc.sync.dma_start(out[h * HALF : (h + 1) * HALF, :], y[h][:])

@@ -25,6 +25,8 @@ HALF = 128
 HALVES = J // HALF
 LEAD = 8
 QUADS = 4
+SIDE = 128
+SIDES = N // SIDE
 
 
 def tile_list_steps_plain_rowshares_kernel(tc, xf, fk, w_words, w_scales, wb_words, wb_scales, bi, offs, out):
@@ -40,7 +42,7 @@ def tile_list_steps_plain_rowshares_kernel(tc, xf, fk, w_words, w_scales, wb_wor
         w_raw = sb.tile([P, R], U16, name="w_raw", tag="words_in", align_bytes=64)
         sc_rows = sb.tile([P, R], U8, name="sc_rows", align_bytes=64)
         zero = sb.tile([P, PACK], F32, name="zero")
-        w_codes = sb.tile([P, R], U16, name="w_codes", align_bytes=64)
+        w_codes = [sb.tile([P, P], U16, name="w_codes%d" % t, align_bytes=64) for t in range(PACK)]
         w_sc = sb.tile([P, R], U8, name="w_sc", align_bytes=64)
         ident = sb.tile([P, P], F32, name="ident", align_bytes=64)
         bias = sb.tile([P, N], F32, name="bias", align_bytes=64)
@@ -60,33 +62,29 @@ def tile_list_steps_plain_rowshares_kernel(tc, xf, fk, w_words, w_scales, wb_wor
         total = [sb.tile([P, 1], F32, name="total%d" % h) for h in range(HALVES)]
         inv = [sb.tile([P, 1], F32, name="inv%d" % h) for h in range(HALVES)]
         bias_ps = ps.tile([P, 2, P], F32, name="bias_ps")
-        a_ps = [ps.tile([P, PACK, HALF], F32, name="a_ps%d" % h) for h in range(HALVES)]
-        p_ps = [ps.tile([P, N], F32, name="p_ps%d" % h) for h in range(HALVES)]
+        a_ps = [[ps.tile([P, 2, HALF], F32, name="a_ps%d%d" % (h, e), tag="bank%d%d" % (h, e)) for e in range(2)] for h in range(HALVES)]
 
         xf_planes = xf.rearrange("(p t) n -> t p n", t=PACK)
 
-        nc.vector.memset(sc_rows[:].bitcast(I32), 0)
+        nc.gpsimd.memset(sc_rows[:].bitcast(I32), 0)
         nc.vector.memset(zero[:], 0.0)
 
         nc.sync.dma_start(offsets[:], offs)
         nc.scalar.dma_start(fk_sb[:], fk.rearrange("(p t) o -> p (t o)", t=PACK))
-        nc.sync.dma_start(w_raw[:].bitcast(I32), w_words[0].bitcast(I32))
         nc.sync.dma_start(planes[0][:], xf_planes[0])
-        nc.sync.dma_start(planes[1][:], xf_planes[1])
         for q in range(QUADS):
             nc.sync.dma_start(sc_rows[32 * q : 32 * q + 4, :].bitcast(I32), w_scales[0, 4 * q : 4 * q + 4, :].bitcast(I32))
-        for t in range(2, PACK):
+        for t in range(1, PACK):
             nc.sync.dma_start(planes[t][:], xf_planes[t])
+        nc.sync.dma_start(w_raw[:].bitcast(I32), w_words[0].bitcast(I32))
         nc.sync.dma_start(bi_col[:], bi.rearrange("o (p c) -> (o p) c", c=2))
 
         nc.scalar.activation(picked_all[:, :, LEAD - 1], zero[:], ACT.Copy)
         make_identity(nc, ident[:])
 
-        nc.vector.tensor_copy(w_codes[:].rearrange("p (t m) -> p t m", t=PACK), w_raw[:].rearrange("p (m t) -> p t m", t=PACK))
         nc.vector.tensor_copy(w_sc[:].rearrange("p (t m) -> p t m", t=PACK), sc_rows[:].rearrange("p (m t) -> p t m", t=PACK))
 
-        wb_codes = sb.tile([P, N], U32, name="wb_codes", tag="words_in", align_bytes=64)
-        wb_sc = sc_rows[:, 0:N]
+        wb_codes = sb.tile([P, N], U32, name="wb_codes", align_bytes=64)
         nc.sync.dma_start(wb_codes[:].bitcast(I32), wb_words[0].rearrange("p n t -> p (n t)").bitcast(I32))
         for q in range(QUADS):
             nc.sync.dma_start(sc_rows[32 * q : 32 * q + 4, 0:N].bitcast(I32), wb_scales[0, 4 * q : 4 * q + 4, :].bitcast(I32))
@@ -94,13 +92,11 @@ def tile_list_steps_plain_rowshares_kernel(tc, xf, fk, w_words, w_scales, wb_wor
         for c in range(2):
             nc.tensor.transpose(bias_ps[:, c, :], bi_col[:, c : c + 1].to_broadcast([P, P]), ident[:])
 
-        def gather(t, engine, lo, hi):
-            dst = picked[t][:, LEAD + lo : LEAD + hi]
-            src = planes[t][:].indirect(offsets[:, lo // 16 : hi // 16])
-            if engine == "scalar":
-                nc.scalar.activation(dst, src, ACT.Copy)
-            else:
-                nc.vector.tensor_copy(dst, src)
+        def gather(t, h):
+            cols = HALF // 16
+            dst = picked[t][:, LEAD + h * HALF : LEAD + (h + 1) * HALF]
+            src = planes[t][:].indirect(offsets[:, h * cols : (h + 1) * cols])
+            nc.scalar.activation(dst, src, ACT.Copy)
 
         def take_steps(t, lo, hi):
             nc.vector.scalar_tensor_tensor(
@@ -112,40 +108,47 @@ def tile_list_steps_plain_rowshares_kernel(tc, xf, fk, w_words, w_scales, wb_wor
                 u_bf[h][:].rearrange("p (j t) -> p j t", t=PACK)[:, :, t], steps[t][:, h * HALF : (h + 1) * HALF],
                 fk_sb[:, t : t + 1], None, ALU.mult)
 
-        for t in range(PACK - 1):
-            gather(t, "scalar", 0, J)
-            take_steps(t, 0, J)
+        for t in range(PACK):
+            for h in range(HALVES):
+                gather(t, h)
+            for h in range(HALVES):
+                take_steps(t, h * HALF, (h + 1) * HALF)
             for h in range(HALVES):
                 scale_round(t, h)
-        last = PACK - 1
-        gather(last, "vector", 0, HALF)
-        gather(last, "scalar", HALF, J)
         nc.scalar.copy(bias[:].rearrange("p (n c) -> p n c", c=2), bias_ps[:].rearrange("p c n -> p n c"))
         for h in range(HALVES):
-            take_steps(last, h * HALF, (h + 1) * HALF)
-        for h in range(HALVES):
-            scale_round(last, h)
-        for h in range(HALVES):
             nc.vector.quantize_mx(out=u_codes[h][:].bitcast(E4M3X4), scales=u_sc[h][:], in_=u_bf[h][:])
+        for t in range(PACK):
+            nc.vector.tensor_copy(w_codes[t][:], w_raw[:].rearrange("p (m t) -> p t m", t=PACK)[:, t, :])
         for h in range(HALVES):
             for t in range(PACK):
                 cols = slice(t * P, (t + 1) * P)
                 nc.tensor.matmul_mx(
-                    a_ps[h][:, t, :], lhsT=w_codes[:, cols].bitcast(E2M1X4), lhsT_scale=w_sc[:, cols],
+                    a_ps[h][t // 2][:, t % 2, :], lhsT=w_codes[t][:].bitcast(E2M1X4), lhsT_scale=w_sc[:, cols],
                     rhs=u_codes[h][:].bitcast(E4M3X4), rhs_scale=u_sc[h][:], start=True, stop=True)
         for h in range(HALVES):
-            nc.scalar.activation(
-                hid_bf[h][:].rearrange("p (j t) -> p j t", t=PACK), a_ps[h][:].rearrange("p t j -> p j t"), ACT.Relu)
+            woven = hid_bf[h][:].rearrange("p (j t) -> p j t", t=PACK)
+            nc.scalar.activation(woven[:, :, 0:2], a_ps[h][0][:].rearrange("p t j -> p j t"), ACT.Relu)
+            nc.vector.tensor_scalar(woven[:, :, 2:4], a_ps[h][1][:].rearrange("p t j -> p j t"), 0.0, None, ALU.max)
+        p_ps = [[ps.tile([P, SIDE], F32, name="p_ps%d%d" % (h, s), tag=("bias_ps" if h + s == 0 else "p_ps%d%d" % (h, s))) for s in range(SIDES)] for h in range(HALVES)]
         for h in range(HALVES):
             nc.vector.quantize_mx(out=hid_codes[h][:].bitcast(E5M2X4), scales=hid_sc[h][:], in_=hid_bf[h][:])
-            nc.tensor.matmul_mx(
-                p_ps[h][:], lhsT=hid_codes[h][:].bitcast(E5M2X4), lhsT_scale=hid_sc[h][:],
-                rhs=wb_codes[:].bitcast(E5M2X4), rhs_scale=wb_sc, start=True, stop=True)
+            for s in range(SIDES):
+                cols = slice(s * SIDE, (s + 1) * SIDE)
+                nc.tensor.matmul_mx(
+                    p_ps[h][s][:], lhsT=hid_codes[h][:].bitcast(E5M2X4), lhsT_scale=hid_sc[h][:],
+                    rhs=wb_codes[:, cols].bitcast(E5M2X4), rhs_scale=sc_rows[:, cols], start=True, stop=True)
         for h in range(HALVES):
-            nc.vector.scalar_tensor_tensor(neg_z[h][:], p_ps[h][:], -0.7, bias[:], ALU.mult, ALU.subtract)
+            for s in range(SIDES):
+                cols = slice(s * SIDE, (s + 1) * SIDE)
+                nc.vector.scalar_tensor_tensor(neg_z[h][:, cols], p_ps[h][s][:], -0.7, bias[:, cols], ALU.mult, ALU.subtract)
+        for h in range(HALVES):
             nc.vector.tensor_reduce(neg_max[h][:], neg_z[h][:], AXIS.X, ALU.min)
             nc.scalar.activation(ea[h][:], neg_z[h][:], ACT.Exp, bias=neg_max[h][:], scale=-1.0, accum_out=total[h][:])
         for h in range(HALVES):
             nc.vector.reciprocal(inv[h][:], total[h][:])
-            nc.vector.tensor_scalar(y[h][:], ea[h][:], inv[h][:], 256.0, ALU.mult, ALU.mult)
-            nc.sync.dma_start(out[h * HALF : (h + 1) * HALF, :], y[h][:])
+            for s in range(SIDES):
+                cols = slice(s * SIDE, (s + 1) * SIDE)
+                nc.vector.tensor_scalar(y[h][:, cols], ea[h][:, cols], inv[h][:], 256.0, ALU.mult, ALU.mult)
+                queue = nc.sync if s == 0 else nc.scalar
+                queue.dma_start(out[h * HALF : (h + 1) * HALF, cols], y[h][:, cols])

@@ -128,8 +128,8 @@ def tile_list_steps_plain_rowshares_kernel(tc, xf, fk, w_words, w_scales, wb_wor
                     rhs=u_codes[h][:].bitcast(E4M3X4), rhs_scale=u_sc[h][:], start=True, stop=True)
         for h in range(HALVES):
             woven = hid_bf[h][:].rearrange("p (j t) -> p j t", t=PACK)
-            nc.scalar.activation(woven[:, :, 0:2], a_ps[h][0][:].rearrange("p t j -> p j t"), ACT.Relu)
-            nc.vector.tensor_scalar(woven[:, :, 2:4], a_ps[h][1][:].rearrange("p t j -> p j t"), 0.0, None, ALU.max)
+            nc.vector.tensor_scalar(woven[:, :, 0:2], a_ps[h][0][:].rearrange("p t j -> p j t"), 0.0, None, ALU.max)
+            nc.scalar.activation(woven[:, :, 2:4], a_ps[h][1][:].rearrange("p t j -> p j t"), ACT.Relu)
         p_ps = [[ps.tile([P, SIDE], F32, name="p_ps%d%d" % (h, s), tag=("bias_ps" if h + s == 0 else "p_ps%d%d" % (h, s))) for s in range(SIDES)] for h in range(HALVES)]
         for h in range(HALVES):
             nc.vector.quantize_mx(out=hid_codes[h][:].bitcast(E5M2X4), scales=hid_sc[h][:], in_=hid_bf[h][:])

from contextlib import ExitStack

import concourse.mybir as mybir
from concourse.masks import make_identity

K, T, J, R, N = 512, 1024, 256, 512, 256
FLOPS = 2 * K * R * J + 2 * R * J * N

F32 = mybir.dt.float32
BF16 = mybir.dt.bfloat16
I32 = mybir.dt.int32
U32 = mybir.dt.uint32
U16 = mybir.dt.uint16
U8 = mybir.dt.uint8
E4M3X4 = mybir.dt.float8_e4m3fn_x4
E5M2X4 = mybir.dt.float8_e5m2_x4
E2M1X4 = mybir.dt.float4_e2m1fn_x4
ALU = mybir.AluOpType
ACT = mybir.ActivationFunctionType
AXIS = mybir.AxisListType

P = 128
PACK = 4
HALF = 128
HALVES = J // HALF
LEAD = 8
QUADS = 4
SIDE = 128
SIDES = N // SIDE


def tile_list_steps_plain_rowshares_kernel(tc, xf, fk, w_words, w_scales, wb_words, wb_scales, bi, offs, out):
    nc = tc.nc
    with ExitStack() as ctx:
        sb = ctx.enter_context(tc.tile_pool(name="sb", bufs=1))
        ps = ctx.enter_context(tc.psum_pool(name="ps", bufs=1))

        offsets = sb.tile([P, J // 16], U16, name="offsets")
        planes = [sb.tile([P, T], F32, name="plane%d" % t, align_bytes=64) for t in range(PACK)]
        fk_sb = sb.tile([P, PACK], F32, name="fk_sb")
        bi_col = sb.tile([P, 2], F32, name="bi_col")
        w_raw = sb.tile([P, R], U16, name="w_raw", tag="words_in", align_bytes=64)
        sc_rows = sb.tile([P, R], U8, name="sc_rows", align_bytes=64)
        zero = sb.tile([P, PACK], F32, name="zero")
        w_codes = [sb.tile([P, P], U16, name="w_codes%d" % t, align_bytes=64) for t in range(PACK)]
        w_sc = sb.tile([P, R], U8, name="w_sc", align_bytes=64)
        ident = sb.tile([P, P], F32, name="ident", align_bytes=64)
        bias = sb.tile([P, N], F32, name="bias", align_bytes=64)
        picked_all = sb.tile([P, PACK, LEAD + J], F32, name="picked", align_bytes=64)
        picked = [picked_all[:, t, :] for t in range(PACK)]
        steps = [sb.tile([P, J], F32, name="steps%d" % t, align_bytes=64) for t in range(PACK)]
        u_bf = [sb.tile([P, HALF * PACK], BF16, name="u_bf%d" % h, align_bytes=64) for h in range(HALVES)]
        u_codes = [sb.tile([P, HALF], U32, name="u_codes%d" % h, align_bytes=64) for h in range(HALVES)]
        u_sc = [sb.tile([P, HALF], U8, name="u_sc%d" % h, align_bytes=64) for h in range(HALVES)]
        hid_bf = [sb.tile([P, HALF * PACK], BF16, name="hid_bf%d" % h, align_bytes=64) for h in range(HALVES)]
        hid_codes = [sb.tile([P, HALF], U32, name="hid_codes%d" % h, align_bytes=64) for h in range(HALVES)]
        hid_sc = [sb.tile([P, HALF], U8, name="hid_sc%d" % h, align_bytes=64) for h in range(HALVES)]
        neg_z = [sb.tile([P, N], F32, name="neg_z%d" % h, align_bytes=64) for h in range(HALVES)]
        ea = [sb.tile([P, N], F32, name="ea%d" % h, align_bytes=64) for h in range(HALVES)]
        y = [sb.tile([P, N], F32, name="y%d" % h, align_bytes=64) for h in range(HALVES)]
        neg_max = [sb.tile([P, 1], F32, name="neg_max%d" % h) for h in range(HALVES)]
        total = [sb.tile([P, 1], F32, name="total%d" % h) for h in range(HALVES)]
        inv = [sb.tile([P, 1], F32, name="inv%d" % h) for h in range(HALVES)]
        bias_ps = ps.tile([P, 2, P], F32, name="bias_ps")
        a_ps = [[ps.tile([P, 2, HALF], F32, name="a_ps%d%d" % (h, e), tag="bank%d%d" % (h, e)) for e in range(2)] for h in range(HALVES)]

        xf_planes = xf.rearrange("(p t) n -> t p n", t=PACK)

        nc.gpsimd.memset(sc_rows[:].bitcast(I32), 0)
        nc.vector.memset(zero[:], 0.0)

        nc.sync.dma_start(offsets[:], offs)
        nc.scalar.dma_start(fk_sb[:], fk.rearrange("(p t) o -> p (t o)", t=PACK))
        nc.sync.dma_start(planes[0][:], xf_planes[0])
        for q in range(QUADS):
            nc.sync.dma_start(sc_rows[32 * q : 32 * q + 4, :].bitcast(I32), w_scales[0, 4 * q : 4 * q + 4, :].bitcast(I32))
        for t in range(1, PACK):
            nc.sync.dma_start(planes[t][:], xf_planes[t])
        nc.sync.dma_start(w_raw[:].bitcast(I32), w_words[0].bitcast(I32))
        nc.sync.dma_start(bi_col[:], bi.rearrange("o (p c) -> (o p) c", c=2))

        nc.scalar.activation(picked_all[:, :, LEAD - 1], zero[:], ACT.Copy)
        make_identity(nc, ident[:])

        nc.vector.tensor_copy(w_sc[:].rearrange("p (t m) -> p t m", t=PACK), sc_rows[:].rearrange("p (m t) -> p t m", t=PACK))

        wb_codes = sb.tile([P, N], U32, name="wb_codes", align_bytes=64)
        nc.sync.dma_start(wb_codes[:].bitcast(I32), wb_words[0].rearrange("p n t -> p (n t)").bitcast(I32))
        for q in range(QUADS):
            nc.sync.dma_start(sc_rows[32 * q : 32 * q + 4, 0:N].bitcast(I32), wb_scales[0, 4 * q : 4 * q + 4, :].bitcast(I32))

        for c in range(2):
            nc.tensor.transpose(bias_ps[:, c, :], bi_col[:, c : c + 1].to_broadcast([P, P]), ident[:])

        def gather(t, h):
            cols = HALF // 16
            dst = picked[t][:, LEAD + h * HALF : LEAD + (h + 1) * HALF]
            src = planes[t][:].indirect(offsets[:, h * cols : (h + 1) * cols])
            nc.scalar.activation(dst, src, ACT.Copy)

        def take_steps(t, lo, hi):
            nc.vector.scalar_tensor_tensor(
                steps[t][:, lo:hi], picked[t][:, LEAD - 1 + lo : LEAD - 1 + hi], -0.6,
                picked[t][:, LEAD + lo : LEAD + hi], ALU.mult, ALU.add)

        def scale_round(t, h):
            nc.vector.tensor_scalar(
                u_bf[h][:].rearrange("p (j t) -> p j t", t=PACK)[:, :, t], steps[t][:, h * HALF : (h + 1) * HALF],
                fk_sb[:, t : t + 1], None, ALU.mult)

        for t in range(PACK):
            for h in range(HALVES):
                gather(t, h)
            for h in range(HALVES):
                take_steps(t, h * HALF, (h + 1) * HALF)
            for h in range(HALVES):
                scale_round(t, h)
        nc.scalar.copy(bias[:].rearrange("p (n c) -> p n c", c=2), bias_ps[:].rearrange("p c n -> p n c"))
        for h in range(HALVES):
            nc.vector.quantize_mx(out=u_codes[h][:].bitcast(E4M3X4), scales=u_sc[h][:], in_=u_bf[h][:])
        for t in range(PACK):
            nc.vector.tensor_copy(w_codes[t][:], w_raw[:].rearrange("p (m t) -> p t m", t=PACK)[:, t, :])
        for h in range(HALVES):
            for t in range(PACK):
                cols = slice(t * P, (t + 1) * P)
                nc.tensor.matmul_mx(
                    a_ps[h][t // 2][:, t % 2, :], lhsT=w_codes[t][:].bitcast(E2M1X4), lhsT_scale=w_sc[:, cols],
                    rhs=u_codes[h][:].bitcast(E4M3X4), rhs_scale=u_sc[h][:], start=True, stop=True)
        for h in range(HALVES):
            woven = hid_bf[h][:].rearrange("p (j t) -> p j t", t=PACK)
            nc.vector.tensor_scalar(woven[:, :, 0:2], a_ps[h][0][:].rearrange("p t j -> p j t"), 0.0, None, ALU.max)
            nc.scalar.activation(woven[:, :, 2:4], a_ps[h][1][:].rearrange("p t j -> p j t"), ACT.Relu)
        p_ps = [[ps.tile([P, SIDE], F32, name="p_ps%d%d" % (h, s), tag=("bias_ps" if h + s == 0 else "p_ps%d%d" % (h, s))) for s in range(SIDES)] for h in range(HALVES)]
        for h in range(HALVES):
            nc.vector.quantize_mx(out=hid_codes[h][:].bitcast(E5M2X4), scales=hid_sc[h][:], in_=hid_bf[h][:])
            for s in range(SIDES):
                cols = slice(s * SIDE, (s + 1) * SIDE)
                nc.tensor.matmul_mx(
                    p_ps[h][s][:], lhsT=hid_codes[h][:].bitcast(E5M2X4), lhsT_scale=hid_sc[h][:],
                    rhs=wb_codes[:, cols].bitcast(E5M2X4), rhs_scale=sc_rows[:, cols], start=True, stop=True)
        for h in range(HALVES):
            for s in range(SIDES):
                cols = slice(s * SIDE, (s + 1) * SIDE)
                nc.vector.scalar_tensor_tensor(neg_z[h][:, cols], p_ps[h][s][:], -0.7, bias[:, cols], ALU.mult, ALU.subtract)
        for h in range(HALVES):
            nc.vector.tensor_reduce(neg_max[h][:], neg_z[h][:], AXIS.X, ALU.min)
            nc.scalar.activation(ea[h][:], neg_z[h][:], ACT.Exp, bias=neg_max[h][:], scale=-1.0, accum_out=total[h][:])
        for h in range(HALVES):
            nc.vector.reciprocal(inv[h][:], total[h][:])
            for s in range(SIDES):
                cols = slice(s * SIDE, (s + 1) * SIDE)
                nc.vector.tensor_scalar(y[h][:, cols], ea[h][:, cols], inv[h][:], 256.0, ALU.mult, ALU.mult)
                queue = nc.sync if s == 0 else nc.scalar
                queue.dma_start(out[h * HALF : (h + 1) * HALF, cols], y[h][:, cols])
